import numpy as np
import ml_dtypes


def mxq(x, axis, fmt="e4m3"):
    dtype, down = {"e4m3": (ml_dtypes.float8_e4m3fn, 7), "e5m2": (ml_dtypes.float8_e5m2, 14)}[fmt]
    v = np.moveaxis(np.asarray(x, np.float32).astype(ml_dtypes.bfloat16).astype(np.float64), axis, -1)
    blocks = v.reshape(v.shape[:-1] + (-1, 32))
    amax = np.abs(blocks).max(-1, keepdims=True)
    byte = np.maximum(np.where(amax > 0, np.frexp(amax)[1] - 1 + 127, 0) - down, 1)
    scale = np.exp2(byte - 127.0)
    codes = (blocks / scale).astype(np.float32).astype(dtype).astype(np.float64)
    return np.moveaxis((codes * scale).reshape(v.shape), -1, axis)


WIDE = False


def mx_kscale(k):
    if not WIDE:
        return np.ones(k)
    levels = np.array([30, -30])
    if k % 512:
        return np.exp2(np.random.permutation(np.resize(levels, k // 32))).repeat(32)
    a = np.empty((k // 512, 16))
    for p in range(k // 512):
        a[p, :8] = np.random.permutation(np.resize(levels, 8))
        for g in range(8):
            far = levels[np.abs(levels - a[p, g]) >= 10]
            a[p, g + 8] = far[np.random.randint(len(far))]
    return np.exp2(a.ravel()).repeat(32)


def f64(x):
    return np.asarray(x).astype(np.float64)


def striped(idx):
    return np.tile(np.asarray(idx).reshape(-1, 16).T, (8, 1)).astype(np.uint16)


def unstriped(offs):
    return offs[:16].T.reshape(-1).astype(np.int64)


E2M1 = np.array([0.0, 0.5, 1.0, 1.5, 2.0, 3.0, 4.0, 6.0, -0.0, -0.5, -1.0, -1.5, -2.0, -3.0, -4.0, -6.0])


def pack_weight(w, fmt):
    k, n = w.shape
    w = f64(np.asarray(w, np.float32).astype(ml_dtypes.bfloat16)).reshape(k // 32, 32, n)
    amax = np.abs(w).max(1)
    if fmt in ("e4m3", "e5m2"):
        byte = np.frexp(amax)[1] - 1 + 127 - (7 if fmt == "e4m3" else 14)
    else:
        mant, ex = np.frexp(amax / 6.0)
        byte = np.where(mant > 0.5, ex, ex - 1) + 127
    byte = np.clip(np.where(amax > 0, byte, 1), 1, 254)
    scaled = (w * np.exp2(127.0 - byte)[:, None, :]).reshape(k, n).astype(np.float32)
    by_word = np.ascontiguousarray(scaled.reshape(k // 512, 128, 4, n).transpose(0, 1, 3, 2))
    if fmt in ("e4m3", "e5m2"):
        words = by_word.astype(ml_dtypes.float8_e4m3fn if fmt == "e4m3" else ml_dtypes.float8_e5m2).view(np.uint8)
    else:
        c = by_word.astype(ml_dtypes.float4_e2m1fn).view(np.uint8) & 0xF
        words = (c[..., 0::2] | (c[..., 1::2] << 4)).reshape(k // 512, 128, 2 * n)
    return np.ascontiguousarray(words), np.ascontiguousarray(byte.astype(np.uint8).reshape(k // 512, 16, n))


def unpack_weight(words, scales, fmt):
    g, _, n = scales.shape
    words = np.ascontiguousarray(words).reshape(g, 128, n, -1)
    if fmt in ("e4m3", "e5m2"):
        vals = words.view(ml_dtypes.float8_e4m3fn if fmt == "e4m3" else ml_dtypes.float8_e5m2).astype(np.float64)
    else:
        nib = np.empty((g, 128, n, 4), np.uint8)
        nib[..., 0::2] = words & 0xF
        nib[..., 1::2] = words >> 4
        vals = E2M1[nib]
    vals = vals * np.repeat(np.exp2(scales.astype(np.float64) - 127.0), 8, axis=1)[..., None]
    return vals.transpose(0, 1, 3, 2).reshape(g * 512, n)


K, J, N, R, T = 512, 512, 256, 256, 1024


def setup_inputs():
    n = np.random.standard_normal
    idx = np.random.permutation(T)[:J]
    idx2 = np.random.permutation(T)[:J]
    fj = mx_kscale(J)
    fk = mx_kscale(K)
    gjp = pack_weight(n((J, N)) * np.exp(0.5 * n((J, 1))) / fj[:, None], "e5m2")
    drp = pack_weight(n((K, R)) * 1 / np.sqrt(K) / fk[:, None], "e2m1")
    return {
        "xf": (n((K, T))).astype(np.float32),
        "ra": (np.random.uniform(0.5, 1.5, (1, J)) * fj).astype(np.float32),
        "gj_words": gjp[0],
        "gj_scales": gjp[1],
        "fkr": (np.random.uniform(0.5, 1.5, (1, K)) * fk).astype(np.float32),
        "dr_words": drp[0],
        "dr_scales": drp[1],
        "old": (1.0 * n((R, N))).astype(np.float32),
        "offs": striped(idx),
        "offs2": striped(idx2),
    }


def reference(xf, ra, gj_words, gj_scales, fkr, dr_words, dr_scales, old, offs, offs2):
    idx = unstriped(offs)
    idx2 = unstriped(offs2)
    gju = unpack_weight(gj_words, gj_scales, "e5m2")
    dru = unpack_weight(dr_words, dr_scales, "e2m1")
    us = (f64(xf)[:, idx] - f64(xf)[:, idx2]) * f64(ra)
    ut = us.T
    uj = ut * f64(fkr)
    ujq = mxq(uj, 0, "e5m2")
    w = ujq.T @ gju
    wq = mxq(w, 0, "e5m2")
    v2 = dru.T @ wq
    y = 0.05 * v2 + 0.5 * f64(old)
    return y

@@ -1,0 +1,172 @@
+from contextlib import ExitStack
+
+import concourse.mybir as mybir
+
+K, J, N, R, T = 512, 512, 256, 256, 1024
+FLOPS = 2 * J * K * N + 2 * K * R * N
+
+F32 = mybir.dt.float32
+BF16 = mybir.dt.bfloat16
+I32 = mybir.dt.int32
+U32 = mybir.dt.uint32
+U16 = mybir.dt.uint16
+U8 = mybir.dt.uint8
+E5M2 = mybir.dt.float8_e5m2_x4
+E2M1 = mybir.dt.float4_e2m1fn_x4
+MULT = mybir.AluOpType.mult
+ADD = mybir.AluOpType.add
+SUB = mybir.AluOpType.subtract
+COPY = mybir.ActivationFunctionType.Copy
+
+P = 128
+PACK = 4
+QUAD = 32
+HALF = N // 2
+FUSED = 320
+CUTS = (0, 128, FUSED)
+
+
+def tile_list_directions_gaps_stored_mixed_kernel(tc, xf, ra, gj_words, gj_scales, fkr, dr_words, dr_scales, old, offs, offs2, out):
+    nc = tc.nc
+    with ExitStack() as ctx:
+        keep = ctx.enter_context(tc.tile_pool(name="keep", bufs=1))
+        psum = ctx.enter_context(tc.psum_pool(name="psum", bufs=1))
+        turn = ctx.enter_context(tc.psum_pool(name="turn", bufs=4))
+
+        first = keep.tile([P, J // 16], U16, name="first")
+        second = keep.tile([P, J // 16], U16, name="second")
+        x = [keep.tile([P, T], F32, name="x%d" % t) for t in range(PACK)]
+        ra_t = keep.tile([P, PACK], F32, name="ra_t")
+        fk_t = keep.tile([P, PACK], F32, name="fk_t")
+        g_words = keep.tile([P, N], U32, name="g_words", align_bytes=64)
+        d_words = keep.tile([P, 2 * R], U8, name="d_words", align_bytes=64)
+        planes = keep.tile([P, N + R], U8, name="planes", align_bytes=64)
+        old_t = keep.tile([P, 2, N], F32, name="old_t")
+        ident = keep.tile([P, P], F32, name="ident")
+
+        ones = keep.tile([P, QUAD], F32, name="ones")
+        column = keep.tile([P, QUAD], F32, name="column", align_bytes=64)
+        row = keep.tile([P, QUAD], F32, name="row", align_bytes=64)
+        ident_bf = keep.tile([P, P], BF16, name="ident_bf")
+        nc.vector.memset(ones[:], 1.0)
+        nc.vector.memset(ident_bf[:], 0.0)
+        nc.vector.tensor_tensor_scan(column[:], ones[:], ones[:], 0.0, MULT, ADD)
+        nc.vector.memset(planes[:].bitcast(U32), 0)
+        nc.vector.transpose(row[:], column[:])
+        for q in range(P // QUAD):
+            part = slice(q * QUAD, (q + 1) * QUAD)
+            nc.vector.tensor_tensor(ident_bf[part, part], column[part, :], row[part, :], mybir.AluOpType.is_equal)
+
+        x_rows = xf.rearrange("(p t) c -> p t c", t=PACK)
+        nc.sync.dma_start(x[0][:], x_rows[:, 0, :])
+        nc.sync.dma_start(second[:], offs2)
+        nc.sync.dma_start(first[:], offs)
+        nc.sync.dma_start(ra_t[:], ra.rearrange("o (p t) -> (o p) t", t=PACK))
+        nc.sync.dma_start(fk_t[:], fkr.rearrange("o (p t) -> (o p) t", t=PACK))
+        nc.scalar.activation(ident[:], ident_bf[:], COPY)
+        for t in range(1, PACK):
+            nc.sync.dma_start(x[t][:], x_rows[:, t, :])
+        nc.sync.dma_start(g_words[:].bitcast(I32), gj_words[0].rearrange("p n t -> p (n t)").bitcast(I32))
+        for q in range(4):
+            nc.sync.dma_start(planes[32 * q : 32 * q + 4, 0:N].bitcast(I32), gj_scales[0, 4 * q : 4 * q + 4, :].bitcast(I32))
+        nc.sync.dma_start(d_words[:].bitcast(I32), dr_words[0].bitcast(I32))
+        for q in range(4):
+            nc.sync.dma_start(planes[32 * q : 32 * q + 4, N : N + R].bitcast(I32), dr_scales[0, 4 * q : 4 * q + 4, :].bitcast(I32))
+        nc.sync.dma_start(old_t[:], old.rearrange("(b p) n -> p b n", p=P))
+
+        ra_all = psum.tile([P, PACK, P], F32, name="ra_all")
+        for t in range(PACK):
+            nc.tensor.transpose(ra_all[:, t, :], ra_t[:, t : t + 1].to_broadcast([P, P]), ident[:])
+
+        w_bank = [psum.tile([P, PACK, HALF], F32, name="w_bank%d" % h) for h in range(2)]
+
+        def offsets(tile, a, b):
+            return tile[:, a // 16 : b // 16]
+
+        ra_v = ra_all[:].rearrange("p t q -> p q t")
+        pairs = [keep.tile([P, J], BF16, name="pairs%d" % t) for t in range(PACK)]
+
+        def weigh(t, gap, a, b):
+            nc.vector.scalar_tensor_tensor(
+                pairs[t][:, a:b].rearrange("p (q t) -> p q t", t=PACK),
+                gap[:].rearrange("p (q t) -> p q t", t=PACK),
+                fk_t[:, t : t + 1],
+                ra_v[:, a // PACK : b // PACK, :],
+                MULT,
+                MULT,
+            )
+
+        turned = []
+
+        def turn_plane(t):
+            bank = turn.tile([P, 2, P], F32, name="bank")
+            words = pairs[t][:].bitcast(F32)
+            for u in range(2):
+                nc.tensor.transpose(bank[:, u, :], words[:, u :: 2], ident[:])
+            turned.append(bank)
+
+        gap_tail = None
+        for t in range(PACK):
+            minus = keep.tile([P, J], F32, name="minus%d" % t)
+            plus = keep.tile([P, J - FUSED], F32, name="plus%d" % t)
+            gap_head = keep.tile([P, FUSED], F32, name="gap_head")
+            for a, b in zip(CUTS, CUTS[1:]):
+                nc.scalar.activation(minus[:, a:b], x[t][:].indirect(offsets(second, a, b)), COPY)
+                nc.vector.tensor_tensor(gap_head[:, a:b], x[t][:].indirect(offsets(first, a, b)), minus[:, a:b], SUB)
+            nc.scalar.activation(minus[:, FUSED:J], x[t][:].indirect(offsets(second, FUSED, J)), COPY)
+            nc.scalar.activation(plus[:], x[t][:].indirect(offsets(first, FUSED, J)), COPY)
+            if t > 0:
+                weigh(t - 1, gap_tail, FUSED, J)
+                turn_plane(t - 1)
+            weigh(t, gap_head, 0, FUSED)
+            gap_tail = keep.tile([P, J - FUSED], F32, name="gap_tail")
+            nc.vector.tensor_tensor(gap_tail[:], plus[:], minus[:, FUSED:J], SUB)
+        weigh(PACK - 1, gap_tail, FUSED, J)
+        turn_plane(PACK - 1)
+
+        for t in range(PACK):
+            uj = keep.tile([P, P * PACK], BF16, name="uj%d" % t, align_bytes=64)
+            nc.scalar.copy(uj[:].bitcast(F32).rearrange("p (m u) -> p m u", u=2), turned[t][:].rearrange("p u m -> p m u"))
+            u_words = keep.tile([P, P], U32, name="u_words%d" % t, align_bytes=64)
+            u_scales = keep.tile([P, P], U8, name="u_scales%d" % t, align_bytes=64)
+            nc.vector.quantize_mx(u_words[:].bitcast(E5M2), u_scales[:], uj[:])
+            for h in range(2):
+                cols = slice(h * HALF, (h + 1) * HALF)
+                nc.tensor.matmul_mx(
+                    w_bank[h][:, t, :],
+                    lhsT=u_words[:].bitcast(E5M2),
+                    lhsT_scale=u_scales[:],
+                    rhs=g_words[:, cols].bitcast(E5M2),
+                    rhs_scale=planes[:, cols],
+                    start=True,
+                    stop=True,
+                )
+
+        half_old = keep.tile([P, 2, N], F32, name="gap_tail")
+        nc.vector.tensor_scalar_mul(half_old[:], old_t[:], 0.5)
+
+        w_bf = [keep.tile([P, HALF * PACK], BF16, name="w_bf%d" % h, align_bytes=64) for h in range(2)]
+        nc.scalar.copy(w_bf[0][:].rearrange("p (n t) -> p n t", t=PACK), w_bank[0][:].rearrange("p t n -> p n t"))
+        nc.vector.tensor_copy(w_bf[1][:].rearrange("p (n t) -> p n t", t=PACK), w_bank[1][:].rearrange("p t n -> p n t"))
+
+        out_v = out.rearrange("(b p) n -> p b n", p=P)
+        for h in range(2):
+            cols = slice(h * HALF, (h + 1) * HALF)
+            w_words = keep.tile([P, HALF], U32, name="w_words%d" % h, align_bytes=64)
+            w_scales = keep.tile([P, HALF], U8, name="w_scales%d" % h, align_bytes=64)
+            nc.vector.quantize_mx(w_words[:].bitcast(E5M2), w_scales[:], w_bf[h][:])
+            v_bank = turn.tile([P, 2, HALF], F32, name="bank")
+            for b in range(2):
+                nc.tensor.matmul_mx(
+                    v_bank[:, b, :],
+                    lhsT=d_words[:, 2 * P * b : 2 * P * (b + 1)].bitcast(E2M1),
+                    lhsT_scale=planes[:, N + P * b : N + P * (b + 1)],
+                    rhs=w_words[:].bitcast(E5M2),
+                    rhs_scale=w_scales[:],
+                    start=True,
+                    stop=True,
+                )
+            result = keep.tile([P, 2, HALF], F32, name="result%d" % h)
+            nc.vector.scalar_tensor_tensor(result[:], v_bank[:], 0.05, half_old[:, :, cols], MULT, ADD)
+            queue = nc.sync if h == 0 else nc.scalar
+            queue.dma_start(out_v[:, :, cols], result[:])

@@ -23,7 +23,7 @@ PACK = 4
 QUAD = 32
 HALF = N // 2
 FUSED = 320
-CUTS = (0, 128, FUSED)
+FIRST_CUTS = (0, 128, FUSED)
 
 
 def tile_list_directions_gaps_stored_mixed_kernel(tc, xf, ra, gj_words, gj_scales, fkr, dr_words, dr_scales, old, offs, offs2, out):
@@ -96,53 +96,78 @@ def tile_list_directions_gaps_stored_mixed_kernel(tc, xf, ra, gj_words, gj_scale
                 MULT,
             )
 
+        def weigh_last(gap, a, b):
+            t = PACK - 1
+            for u in range(2):
+                nc.vector.scalar_tensor_tensor(
+                    pairs[t][:].rearrange("p (u q e) -> p u q e", u=2, e=2)[:, u, a // PACK : b // PACK, :],
+                    gap[:].rearrange("p (q u e) -> p u q e", u=2, e=2)[:, u],
+                    fk_t[:, t : t + 1],
+                    ra_v[:, a // PACK : b // PACK, 2 * u : 2 * u + 2],
+                    MULT,
+                    MULT,
+                )
+
         turned = []
 
         def turn_plane(t):
             bank = turn.tile([P, 2, P], F32, name="bank")
             words = pairs[t][:].bitcast(F32)
             for u in range(2):
-                nc.tensor.transpose(bank[:, u, :], words[:, u :: 2], ident[:])
+                picked = words[:, u :: 2] if t < PACK - 1 else words[:, u * P : (u + 1) * P]
+                nc.tensor.transpose(bank[:, u, :], picked, ident[:])
             turned.append(bank)
 
         gap_tail = None
         for t in range(PACK):
-            minus = keep.tile([P, J], F32, name="minus%d" % t)
+            minus_head = keep.tile([P, FUSED], F32, name="minus_head%d" % t, align_bytes=64)
+            minus_tail = keep.tile([P, J - FUSED], F32, name="minus_tail%d" % t)
+            cuts = FIRST_CUTS if t == 0 else (0, FUSED)
             plus = keep.tile([P, J - FUSED], F32, name="plus%d" % t)
-            gap_head = keep.tile([P, FUSED], F32, name="gap_head")
-            for a, b in zip(CUTS, CUTS[1:]):
-                nc.scalar.activation(minus[:, a:b], x[t][:].indirect(offsets(second, a, b)), COPY)
-                nc.vector.tensor_tensor(gap_head[:, a:b], x[t][:].indirect(offsets(first, a, b)), minus[:, a:b], SUB)
-            nc.scalar.activation(minus[:, FUSED:J], x[t][:].indirect(offsets(second, FUSED, J)), COPY)
+            gap_head = keep.tile([P, FUSED], F32, name="gap_head", align_bytes=64)
+            for a, b in zip(cuts, cuts[1:]):
+                nc.scalar.activation(minus_head[:, a:b], x[t][:].indirect(offsets(second, a, b)), COPY)
+                nc.vector.tensor_tensor(gap_head[:, a:b], x[t][:].indirect(offsets(first, a, b)), minus_head[:, a:b], SUB)
+            nc.scalar.activation(minus_tail[:], x[t][:].indirect(offsets(second, FUSED, J)), COPY)
             nc.scalar.activation(plus[:], x[t][:].indirect(offsets(first, FUSED, J)), COPY)
             if t > 0:
                 weigh(t - 1, gap_tail, FUSED, J)
                 turn_plane(t - 1)
-            weigh(t, gap_head, 0, FUSED)
-            gap_tail = keep.tile([P, J - FUSED], F32, name="gap_tail")
-            nc.vector.tensor_tensor(gap_tail[:], plus[:], minus[:, FUSED:J], SUB)
-        weigh(PACK - 1, gap_tail, FUSED, J)
+            if t < PACK - 1:
+                weigh(t, gap_head, 0, FUSED)
+                gap_tail = keep.tile([P, J - FUSED], F32, name="gap_tail")
+                nc.vector.tensor_tensor(gap_tail[:], plus[:], minus_tail[:], SUB)
+            else:
+                gap_tail = keep.tile([P, J - FUSED], F32, name="gap_last")
+                weigh_last(gap_head, 0, FUSED)
+                nc.vector.tensor_tensor(gap_tail[:], plus[:], minus_tail[:], SUB)
+        weigh_last(gap_tail, FUSED, J)
         turn_plane(PACK - 1)
 
+        early = keep.tile([P, 2 * J], BF16, name="minus_head%d" % (PACK - 1), align_bytes=64)
+        third = keep.tile([P, J], BF16, name="gap_head", align_bytes=64)
+        last = keep.tile([P, J], BF16, name="last", align_bytes=64)
+        u_words = keep.tile([P, PACK * P], U32, name="u_words", align_bytes=64)
+        u_scales = keep.tile([P, PACK * P], U8, name="u_scales", align_bytes=64)
+        for t, uj in enumerate((early[:, 0:J], early[:, J : 2 * J], third[:], last[:])):
+            move = nc.vector.tensor_copy if t == 2 else nc.scalar.copy
+            move(uj.bitcast(F32).rearrange("p (m u) -> p m u", u=2), turned[t][:].rearrange("p u m -> p m u"))
+        for a, b, uj in ((0, 2, early[:]), (2, 3, third[:]), (3, 4, last[:])):
+            nc.vector.quantize_mx(u_words[:, a * P : b * P].bitcast(E5M2), u_scales[:, a * P : b * P], uj)
         for t in range(PACK):
-            uj = keep.tile([P, P * PACK], BF16, name="uj%d" % t, align_bytes=64)
-            nc.scalar.copy(uj[:].bitcast(F32).rearrange("p (m u) -> p m u", u=2), turned[t][:].rearrange("p u m -> p m u"))
-            u_words = keep.tile([P, P], U32, name="u_words%d" % t, align_bytes=64)
-            u_scales = keep.tile([P, P], U8, name="u_scales%d" % t, align_bytes=64)
-            nc.vector.quantize_mx(u_words[:].bitcast(E5M2), u_scales[:], uj[:])
             for h in range(2):
                 cols = slice(h * HALF, (h + 1) * HALF)
                 nc.tensor.matmul_mx(
                     w_bank[h][:, t, :],
-                    lhsT=u_words[:].bitcast(E5M2),
-                    lhsT_scale=u_scales[:],
+                    lhsT=u_words[:, t * P : (t + 1) * P].bitcast(E5M2),
+                    lhsT_scale=u_scales[:, t * P : (t + 1) * P],
                     rhs=g_words[:, cols].bitcast(E5M2),
                     rhs_scale=planes[:, cols],
                     start=True,
                     stop=True,
                 )
 
-        half_old = keep.tile([P, 2, N], F32, name="gap_tail")
+        half_old = keep.tile([P, 2, N], F32, name="last", align_bytes=64)
         nc.vector.tensor_scalar_mul(half_old[:], old_t[:], 0.5)
 
         w_bf = [keep.tile([P, HALF * PACK], BF16, name="w_bf%d" % h, align_bytes=64) for h in range(2)]

from contextlib import ExitStack

import concourse.mybir as mybir

K, J, N, R, T = 512, 512, 256, 256, 1024
FLOPS = 2 * J * K * N + 2 * K * R * N

F32 = mybir.dt.float32
BF16 = mybir.dt.bfloat16
I32 = mybir.dt.int32
U32 = mybir.dt.uint32
U16 = mybir.dt.uint16
U8 = mybir.dt.uint8
E5M2 = mybir.dt.float8_e5m2_x4
E2M1 = mybir.dt.float4_e2m1fn_x4
MULT = mybir.AluOpType.mult
ADD = mybir.AluOpType.add
SUB = mybir.AluOpType.subtract
COPY = mybir.ActivationFunctionType.Copy

P = 128
PACK = 4
QUAD = 32
HALF = N // 2
FUSED = 320
FIRST_CUTS = (0, 128, FUSED)


def tile_list_directions_gaps_stored_mixed_kernel(tc, xf, ra, gj_words, gj_scales, fkr, dr_words, dr_scales, old, offs, offs2, out):
    nc = tc.nc
    with ExitStack() as ctx:
        keep = ctx.enter_context(tc.tile_pool(name="keep", bufs=1))
        psum = ctx.enter_context(tc.psum_pool(name="psum", bufs=1))
        turn = ctx.enter_context(tc.psum_pool(name="turn", bufs=4))

        first = keep.tile([P, J // 16], U16, name="first")
        second = keep.tile([P, J // 16], U16, name="second")
        x = [keep.tile([P, T], F32, name="x%d" % t) for t in range(PACK)]
        ra_t = keep.tile([P, PACK], F32, name="ra_t")
        fk_t = keep.tile([P, PACK], F32, name="fk_t")
        g_words = keep.tile([P, N], U32, name="g_words", align_bytes=64)
        d_words = keep.tile([P, 2 * R], U8, name="d_words", align_bytes=64)
        planes = keep.tile([P, N + R], U8, name="planes", align_bytes=64)
        old_t = keep.tile([P, 2, N], F32, name="old_t")
        ident = keep.tile([P, P], F32, name="ident")

        ones = keep.tile([P, QUAD], F32, name="ones")
        column = keep.tile([P, QUAD], F32, name="column", align_bytes=64)
        row = keep.tile([P, QUAD], F32, name="row", align_bytes=64)
        ident_bf = keep.tile([P, P], BF16, name="ident_bf")
        nc.vector.memset(ones[:], 1.0)
        nc.vector.memset(ident_bf[:], 0.0)
        nc.vector.tensor_tensor_scan(column[:], ones[:], ones[:], 0.0, MULT, ADD)
        nc.vector.memset(planes[:].bitcast(U32), 0)
        nc.vector.transpose(row[:], column[:])
        for q in range(P // QUAD):
            part = slice(q * QUAD, (q + 1) * QUAD)
            nc.vector.tensor_tensor(ident_bf[part, part], column[part, :], row[part, :], mybir.AluOpType.is_equal)

        x_rows = xf.rearrange("(p t) c -> p t c", t=PACK)
        nc.sync.dma_start(x[0][:], x_rows[:, 0, :])
        nc.sync.dma_start(second[:], offs2)
        nc.sync.dma_start(first[:], offs)
        nc.sync.dma_start(ra_t[:], ra.rearrange("o (p t) -> (o p) t", t=PACK))
        nc.sync.dma_start(fk_t[:], fkr.rearrange("o (p t) -> (o p) t", t=PACK))
        nc.scalar.activation(ident[:], ident_bf[:], COPY)
        for t in range(1, PACK):
            nc.sync.dma_start(x[t][:], x_rows[:, t, :])
        nc.sync.dma_start(g_words[:].bitcast(I32), gj_words[0].rearrange("p n t -> p (n t)").bitcast(I32))
        for q in range(4):
            nc.sync.dma_start(planes[32 * q : 32 * q + 4, 0:N].bitcast(I32), gj_scales[0, 4 * q : 4 * q + 4, :].bitcast(I32))
        nc.sync.dma_start(d_words[:].bitcast(I32), dr_words[0].bitcast(I32))
        for q in range(4):
            nc.sync.dma_start(planes[32 * q : 32 * q + 4, N : N + R].bitcast(I32), dr_scales[0, 4 * q : 4 * q + 4, :].bitcast(I32))
        nc.sync.dma_start(old_t[:], old.rearrange("(b p) n -> p b n", p=P))

        ra_all = psum.tile([P, PACK, P], F32, name="ra_all")
        for t in range(PACK):
            nc.tensor.transpose(ra_all[:, t, :], ra_t[:, t : t + 1].to_broadcast([P, P]), ident[:])

        w_bank = [psum.tile([P, PACK, HALF], F32, name="w_bank%d" % h) for h in range(2)]

        def offsets(tile, a, b):
            return tile[:, a // 16 : b // 16]

        ra_v = ra_all[:].rearrange("p t q -> p q t")
        pairs = [keep.tile([P, J], BF16, name="pairs%d" % t) for t in range(PACK)]

        def weigh(t, gap, a, b):
            nc.vector.scalar_tensor_tensor(
                pairs[t][:, a:b].rearrange("p (q t) -> p q t", t=PACK),
                gap[:].rearrange("p (q t) -> p q t", t=PACK),
                fk_t[:, t : t + 1],
                ra_v[:, a // PACK : b // PACK, :],
                MULT,
                MULT,
            )

        def weigh_last(gap, a, b):
            t = PACK - 1
            for u in range(2):
                nc.vector.scalar_tensor_tensor(
                    pairs[t][:].rearrange("p (u q e) -> p u q e", u=2, e=2)[:, u, a // PACK : b // PACK, :],
                    gap[:].rearrange("p (q u e) -> p u q e", u=2, e=2)[:, u],
                    fk_t[:, t : t + 1],
                    ra_v[:, a // PACK : b // PACK, 2 * u : 2 * u + 2],
                    MULT,
                    MULT,
                )

        turned = []

        def turn_plane(t):
            bank = turn.tile([P, 2, P], F32, name="bank")
            words = pairs[t][:].bitcast(F32)
            for u in range(2):
                picked = words[:, u :: 2] if t < PACK - 1 else words[:, u * P : (u + 1) * P]
                nc.tensor.transpose(bank[:, u, :], picked, ident[:])
            turned.append(bank)

        gap_tail = None
        for t in range(PACK):
            minus_head = keep.tile([P, FUSED], F32, name="minus_head%d" % t, align_bytes=64)
            minus_tail = keep.tile([P, J - FUSED], F32, name="minus_tail%d" % t)
            cuts = FIRST_CUTS if t == 0 else (0, FUSED)
            plus = keep.tile([P, J - FUSED], F32, name="plus%d" % t)
            gap_head = keep.tile([P, FUSED], F32, name="gap_head", align_bytes=64)
            for a, b in zip(cuts, cuts[1:]):
                nc.scalar.activation(minus_head[:, a:b], x[t][:].indirect(offsets(second, a, b)), COPY)
                nc.vector.tensor_tensor(gap_head[:, a:b], x[t][:].indirect(offsets(first, a, b)), minus_head[:, a:b], SUB)
            nc.scalar.activation(minus_tail[:], x[t][:].indirect(offsets(second, FUSED, J)), COPY)
            nc.scalar.activation(plus[:], x[t][:].indirect(offsets(first, FUSED, J)), COPY)
            if t > 0:
                weigh(t - 1, gap_tail, FUSED, J)
                turn_plane(t - 1)
            if t < PACK - 1:
                weigh(t, gap_head, 0, FUSED)
                gap_tail = keep.tile([P, J - FUSED], F32, name="gap_tail")
                nc.vector.tensor_tensor(gap_tail[:], plus[:], minus_tail[:], SUB)
            else:
                gap_tail = keep.tile([P, J - FUSED], F32, name="gap_last")
                weigh_last(gap_head, 0, FUSED)
                nc.vector.tensor_tensor(gap_tail[:], plus[:], minus_tail[:], SUB)
        weigh_last(gap_tail, FUSED, J)
        turn_plane(PACK - 1)

        early = keep.tile([P, 2 * J], BF16, name="minus_head%d" % (PACK - 1), align_bytes=64)
        third = keep.tile([P, J], BF16, name="gap_head", align_bytes=64)
        last = keep.tile([P, J], BF16, name="last", align_bytes=64)
        u_words = keep.tile([P, PACK * P], U32, name="u_words", align_bytes=64)
        u_scales = keep.tile([P, PACK * P], U8, name="u_scales", align_bytes=64)
        for t, uj in enumerate((early[:, 0:J], early[:, J : 2 * J], third[:], last[:])):
            move = nc.vector.tensor_copy if t == 2 else nc.scalar.copy
            move(uj.bitcast(F32).rearrange("p (m u) -> p m u", u=2), turned[t][:].rearrange("p u m -> p m u"))
        for a, b, uj in ((0, 2, early[:]), (2, 3, third[:]), (3, 4, last[:])):
            nc.vector.quantize_mx(u_words[:, a * P : b * P].bitcast(E5M2), u_scales[:, a * P : b * P], uj)
        for t in range(PACK):
            for h in range(2):
                cols = slice(h * HALF, (h + 1) * HALF)
                nc.tensor.matmul_mx(
                    w_bank[h][:, t, :],
                    lhsT=u_words[:, t * P : (t + 1) * P].bitcast(E5M2),
                    lhsT_scale=u_scales[:, t * P : (t + 1) * P],
                    rhs=g_words[:, cols].bitcast(E5M2),
                    rhs_scale=planes[:, cols],
                    start=True,
                    stop=True,
                )

        half_old = keep.tile([P, 2, N], F32, name="last", align_bytes=64)
        nc.vector.tensor_scalar_mul(half_old[:], old_t[:], 0.5)

        w_bf = [keep.tile([P, HALF * PACK], BF16, name="w_bf%d" % h, align_bytes=64) for h in range(2)]
        nc.scalar.copy(w_bf[0][:].rearrange("p (n t) -> p n t", t=PACK), w_bank[0][:].rearrange("p t n -> p n t"))
        nc.vector.tensor_copy(w_bf[1][:].rearrange("p (n t) -> p n t", t=PACK), w_bank[1][:].rearrange("p t n -> p n t"))

        out_v = out.rearrange("(b p) n -> p b n", p=P)
        for h in range(2):
            cols = slice(h * HALF, (h + 1) * HALF)
            w_words = keep.tile([P, HALF], U32, name="w_words%d" % h, align_bytes=64)
            w_scales = keep.tile([P, HALF], U8, name="w_scales%d" % h, align_bytes=64)
            nc.vector.quantize_mx(w_words[:].bitcast(E5M2), w_scales[:], w_bf[h][:])
            v_bank = turn.tile([P, 2, HALF], F32, name="bank")
            for b in range(2):
                nc.tensor.matmul_mx(
                    v_bank[:, b, :],
                    lhsT=d_words[:, 2 * P * b : 2 * P * (b + 1)].bitcast(E2M1),
                    lhsT_scale=planes[:, N + P * b : N + P * (b + 1)],
                    rhs=w_words[:].bitcast(E5M2),
                    rhs_scale=w_scales[:],
                    start=True,
                    stop=True,
                )
            result = keep.tile([P, 2, HALF], F32, name="result%d" % h)
            nc.vector.scalar_tensor_tensor(result[:], v_bank[:], 0.05, half_old[:, :, cols], MULT, ADD)
            queue = nc.sync if h == 0 else nc.scalar
            queue.dma_start(out_v[:, :, cols], result[:])
